import numpy as np
import ml_dtypes


def mxq(x, axis, fmt="e4m3"):
    dtype, down = {"e4m3": (ml_dtypes.float8_e4m3fn, 7), "e5m2": (ml_dtypes.float8_e5m2, 14)}[fmt]
    v = np.moveaxis(np.asarray(x, np.float32).astype(ml_dtypes.bfloat16).astype(np.float64), axis, -1)
    blocks = v.reshape(v.shape[:-1] + (-1, 32))
    amax = np.abs(blocks).max(-1, keepdims=True)
    byte = np.maximum(np.where(amax > 0, np.frexp(amax)[1] - 1 + 127, 0) - down, 1)
    scale = np.exp2(byte - 127.0)
    codes = (blocks / scale).astype(np.float32).astype(dtype).astype(np.float64)
    return np.moveaxis((codes * scale).reshape(v.shape), -1, axis)


WIDE = False


def mx_kscale(k):
    if not WIDE:
        return np.ones(k)
    levels = np.array([10, -10, 5, -5, 0])
    if k % 512:
        return np.exp2(np.random.permutation(np.resize(levels, k // 32))).repeat(32)
    a = np.empty((k // 512, 16))
    for p in range(k // 512):
        a[p, :8] = np.random.permutation(np.resize(levels, 8))
        for g in range(8):
            far = levels[np.abs(levels - a[p, g]) >= 10]
            a[p, g + 8] = far[np.random.randint(len(far))]
    return np.exp2(a.ravel()).repeat(32)


def f64(x):
    return np.asarray(x).astype(np.float64)


def striped(idx):
    return np.tile(idx.reshape(-1, 16).T, (8, 1)).astype(np.uint16)


def unstriped(offs):
    return offs[:16].T.reshape(-1).astype(np.int64)


def pack_weight(w):
    k, n = w.shape
    w = f64(np.asarray(w, np.float32).astype(ml_dtypes.bfloat16)).reshape(k // 32, 32, n)
    amax = np.abs(w).max(1)
    byte = np.clip(np.where(amax > 0, np.frexp(amax)[1] - 1 + 127 - 7, 1), 1, 254)
    scaled = (w * np.exp2(127.0 - byte)[:, None, :]).reshape(k, n).astype(np.float32)
    words = np.ascontiguousarray(scaled.reshape(k // 512, 128, 4, n).transpose(0, 1, 3, 2)).astype(ml_dtypes.float8_e4m3fn).view(np.uint8)
    return words, np.ascontiguousarray(byte.astype(np.uint8).reshape(k // 512, 16, n))


def unpack_weight(words, scales):
    g, p, n, _ = words.shape
    vals = np.ascontiguousarray(words).view(ml_dtypes.float8_e4m3fn).astype(np.float64) * np.repeat(np.exp2(scales.astype(np.float64) - 127.0), 8, axis=1)[..., None]
    return vals.transpose(0, 1, 3, 2).reshape(g * 512, n)


def planes(y):
    n, m = y.shape
    v = y.astype(np.float32).astype(ml_dtypes.bfloat16).astype(np.float64).reshape(n // 32, 32, m)
    top = np.abs(v).max(1)
    byte = np.clip(np.where(top > 0, np.frexp(top)[1] - 1 + 127 - 7, 1), 1, 254)
    codes = (v * np.exp2(127.0 - byte)[:, None, :]).reshape(n, m).astype(np.float32).astype(ml_dtypes.float8_e4m3fn).view(np.uint8)
    words = codes.reshape(n // 512, 128, 4, m).transpose(0, 1, 3, 2)
    return np.ascontiguousarray(words), np.ascontiguousarray(byte.astype(np.uint8).reshape(n // 512, 16, m))


def relu(v):
    return np.maximum(v, 0.0)


def sigmoid(v):
    return 1.0 / (1.0 + np.exp(-np.maximum(v, -700.0)))


K, T, S, W, H = 1024, 1024, 512, 1024, 512


def setup_inputs():
    n = np.random.standard_normal
    s = mx_kscale(K)[:, None]
    u = mx_kscale(H)
    packed_xT = pack_weight(n((K, T)) * s)
    packed_eT = pack_weight(n((K, W)) * s)
    return {
        "x_words": packed_xT[0],
        "x_scales": packed_xT[1],
        "e_words": packed_eT[0],
        "e_scales": packed_eT[1],
        "w1": (n((K, H)) / np.sqrt(2 * K) / s * u).astype(np.float32),
        "w2": (n((K, H)) / np.sqrt(2 * K) / s * u).astype(np.float32),
        "w3": (n((H, H)) / np.sqrt(H) / u[:, None]).astype(np.float32),
        "skip": (n((H, S)) * u[:, None]).astype(np.float32),
        "offs": striped(np.random.permutation(T)[:S]),
        "tok": striped(np.random.permutation(W)[:S]),
    }


def reference(x_words, x_scales, e_words, e_scales, w1, w2, w3, skip, offs, tok):
    xq = unpack_weight(x_words, x_scales)[:, unstriped(offs)]
    e_tok = unpack_weight(e_words, e_scales)[:, unstriped(tok)]
    h = relu(mxq(f64(w1), 0, "e4m3").T @ xq + mxq(f64(w2), 0, "e4m3").T @ e_tok)
    g = sigmoid(mxq(f64(w3), 0, "e4m3").T @ mxq(h, 0, "e4m3"))
    out_0 = f64(skip) + g * (h - f64(skip))
    return (out_0,) + planes(out_0)

@@ -1,0 +1,224 @@
+from contextlib import ExitStack
+
+import concourse.mybir as mybir
+
+K, T, S, H = 1024, 1024, 512, 512
+FLOPS = 2 * (2 * K * H * S + H * H * S)
+
+F32 = mybir.dt.float32
+BF16 = mybir.dt.bfloat16
+I32 = mybir.dt.int32
+U32 = mybir.dt.uint32
+U16 = mybir.dt.uint16
+U8 = mybir.dt.uint8
+FP8X4 = mybir.dt.float8_e4m3fn_x4
+ACT = mybir.ActivationFunctionType
+ALU = mybir.AluOpType
+
+P = 128
+PACK = 4
+K_PASS = P * PACK
+PASSES = K // K_PASS
+CHUNK = 128
+CHUNKS = S // CHUNK
+LIST_ROWS = 16
+SCALAR_SHARE = 48
+
+
+def tile_picked_zhwy_relu_po_kernel(
+    tc, x_words, x_scales, e_words, e_scales, w1, w2, w3, skip, offs, tok, out_0, out_1, out_2
+):
+    nc = tc.nc
+    with ExitStack() as ctx:
+        sb = ctx.enter_context(tc.tile_pool(name="sb", bufs=1))
+        psum = ctx.enter_context(tc.psum_pool(name="psum", bufs=1))
+
+        def load_list(name, src):
+            lst = sb.tile([P, S // LIST_ROWS], U16, name=name)
+            nc.sync.dma_start(lst[:], src)
+            return lst
+
+        def load_words(name, words, o):
+            table = sb.tile([P, T], I32, name=name, align_bytes=64)
+            nc.sync.dma_start(table[:], words[o].rearrange("p n t -> p (n t)").bitcast(I32))
+            return table
+
+        def load_scales(name, scales):
+            table = sb.tile([P, T], U8, name=name, align_bytes=64)
+            nc.gpsimd.memset(table[:].bitcast(I32), 0)
+            for q in range(4):
+                nc.sync.dma_start(
+                    table[32 * q : 32 * q + 4 * PASSES, :].bitcast(I32),
+                    scales.bitcast(I32)[:, 4 * q : 4 * q + 4, :],
+                )
+            return table
+
+        def load_weight(name, w, o):
+            raw = sb.tile([P, PACK, H], F32, name=name, align_bytes=64)
+            nc.sync.dma_start(raw[:], w[o * K_PASS : (o + 1) * K_PASS, :].rearrange("(p j) c -> p j c", j=PACK))
+            return raw
+
+        def load_skip(half):
+            width = S // 2
+            carried = sb.tile([P, PACK, width], F32, name="skip%d" % half, align_bytes=64)
+            nc.sync.dma_start(
+                carried[:], skip[:, half * width : (half + 1) * width].rearrange("(p t) j -> p t j", t=PACK)
+            )
+            return carried
+
+        def gather(name, table, lst, dtype, pieces):
+            picked = sb.tile([P, S], dtype, name=name, align_bytes=64)
+            width = S // pieces
+            cols = width // LIST_ROWS
+            for c in range(pieces):
+                nc.vector.tensor_copy(
+                    picked[:, c * width : (c + 1) * width],
+                    table[:].bitcast(dtype).indirect(lst[:, c * cols : (c + 1) * cols]),
+                )
+            return picked
+
+        def quantize_weight(name, raw, scalar_share):
+            grouped = sb.tile([P, PACK, P, PACK], BF16, name=name + "_bf16", align_bytes=64)
+            codes = sb.tile([P, H], U32, name=name + "_codes", align_bytes=64)
+            scales = sb.tile([P, H], U8, name=name + "_scales", align_bytes=64)
+            src = raw[:].rearrange("p j (m t) -> p m j t", t=PACK)
+            dst = grouped[:].rearrange("p t m j -> p m j t")
+            nc.scalar.copy(dst[:, :scalar_share], src[:, :scalar_share])
+            if scalar_share < P:
+                nc.vector.tensor_copy(dst[:, scalar_share:], src[:, scalar_share:])
+            nc.vector.quantize_mx(codes[:].bitcast(FP8X4), scales[:], grouped[:].rearrange("p t m j -> p (t m j)"))
+            return codes, scales
+
+        warm = sb.tile([P, 8], F32, name="warm")
+        nc.vector.memset(warm[:, 0:1], 0.0)
+        nc.scalar.activation(warm[:, 4:5], warm[:, 0:1], ACT.Sigmoid)
+
+        x_table0 = load_words("x_table0", x_words, 0)
+        offs_list = load_list("offs_list", offs)
+        x_scale_table = load_scales("x_scale_table", x_scales)
+        w1_raw0 = load_weight("w1_raw0", w1, 0)
+        tok_list = load_list("tok_list", tok)
+        e_scale_table = load_scales("e_scale_table", e_scales)
+        x_table1 = load_words("x_table1", x_words, 1)
+        w1_raw1 = load_weight("w1_raw1", w1, 1)
+        e_table0 = load_words("e_table0", e_words, 0)
+        w2_raw0 = load_weight("w2_raw0", w2, 0)
+        w2_raw1 = load_weight("w2_raw1", w2, 1)
+        e_table1 = load_words("e_table1", e_words, 1)
+        w3_raw = load_weight("w3_raw", w3, 0)
+        carried = [load_skip(0), load_skip(1)]
+
+        x_codes0 = gather("x_codes0", x_table0, offs_list, U32, 1)
+        x_picked_scales = gather("x_picked_scales", x_scale_table, offs_list, U8, 1)
+        x_codes1 = gather("x_codes1", x_table1, offs_list, U32, 1)
+        w1_q0 = quantize_weight("w1_0", w1_raw0, P)
+        e_picked_scales = gather("e_picked_scales", e_scale_table, tok_list, U8, 1)
+        e_codes0 = gather("e_codes0", e_table0, tok_list, U32, 1)
+        w1_q1 = quantize_weight("w1_1", w1_raw1, P)
+        w2_q0 = quantize_weight("w2_0", w2_raw0, SCALAR_SHARE)
+        w2_q1 = quantize_weight("w2_1", w2_raw1, SCALAR_SHARE)
+        e_codes1 = gather("e_codes1", e_table1, tok_list, U32, CHUNKS)
+
+        passes = [
+            (w1_q0, x_codes0, x_picked_scales, 0),
+            (w1_q1, x_codes1, x_picked_scales, 1),
+            (w2_q0, e_codes0, e_picked_scales, 0),
+            (w2_q1, e_codes1, e_picked_scales, 1),
+        ]
+
+        y_codes = sb.tile([P, S], U32, name="y_codes", align_bytes=64)
+        y_scales = sb.tile([P, S], U8, name="y_scales", align_bytes=64)
+        out_rows = out_0.rearrange("(p t) j -> p t j", t=PACK)
+        out_words = out_1[0].rearrange("p n t -> p (n t)").bitcast(I32)
+
+        def carried_chunk(c):
+            per_half = CHUNKS // 2
+            return carried[c // per_half][:, :, (c % per_half) * CHUNK : (c % per_half + 1) * CHUNK]
+
+        def hidden(c):
+            cols = slice(c * CHUNK, (c + 1) * CHUNK)
+            acc = psum.tile([P, PACK, CHUNK], F32, name="acc%d" % c)
+            for t in range(PACK):
+                rows = slice(t * P, (t + 1) * P)
+                for i, ((w_codes, w_scales), codes, scales, o) in enumerate(passes):
+                    nc.tensor.matmul_mx(
+                        acc[:, t, :],
+                        lhsT=w_codes[:, rows].bitcast(FP8X4),
+                        lhsT_scale=w_scales[:, rows],
+                        rhs=codes[:, cols].bitcast(FP8X4),
+                        rhs_scale=scales[4 * o :, cols],
+                        start=(i == 0),
+                        stop=(i == len(passes) - 1),
+                    )
+            h_bf16 = sb.tile([P, CHUNK, PACK], BF16, name="h_bf16_%d" % c, align_bytes=64)
+            nc.scalar.activation(h_bf16[:], acc[:].rearrange("p t j -> p j t"), ACT.Relu)
+            h_codes = sb.tile([P, CHUNK], U32, name="h_codes%d" % c, align_bytes=64)
+            h_scales = sb.tile([P, CHUNK], U8, name="h_scales%d" % c, align_bytes=64)
+            nc.vector.quantize_mx(h_codes[:].bitcast(FP8X4), h_scales[:], h_bf16[:].rearrange("p j t -> p (j t)"))
+            return acc, h_codes, h_scales
+
+        def difference(c, acc):
+            diff = sb.tile([P, PACK, CHUNK], F32, name="diff%d" % c, align_bytes=64)
+            nc.vector.scalar_tensor_tensor(diff[:], acc[:], 0.0, carried_chunk(c), ALU.max, ALU.subtract)
+            return diff
+
+        def gate(c, h_codes, h_scales):
+            w_codes, w_scales = w3_q
+            logits = psum.tile([P, PACK, CHUNK], F32, name="logits%d" % c)
+            for t in range(PACK):
+                rows = slice(t * P, (t + 1) * P)
+                nc.tensor.matmul_mx(
+                    logits[:, t, :],
+                    lhsT=w_codes[:, rows].bitcast(FP8X4),
+                    lhsT_scale=w_scales[:, rows],
+                    rhs=h_codes[:].bitcast(FP8X4),
+                    rhs_scale=h_scales[:],
+                    start=True,
+                    stop=True,
+                )
+            g = sb.tile([P, PACK, CHUNK], F32, name="gate%d" % c, align_bytes=64)
+            nc.scalar.activation(g[:], logits[:], ACT.Sigmoid)
+            return g
+
+        def update(c, g, diff):
+            step = sb.tile([P, PACK, CHUNK], F32, name="step%d" % c, align_bytes=64)
+            nc.vector.tensor_tensor(step[:], g[:], diff[:], ALU.mult)
+            return step
+
+        def finish(c, step):
+            cols = slice(c * CHUNK, (c + 1) * CHUNK)
+            y = sb.tile([P, PACK, CHUNK], F32, name="y%d" % c, align_bytes=64)
+            nc.vector.tensor_tensor(y[:], step[:], carried_chunk(c), ALU.add)
+            nc.sync.dma_start(out_rows[:, :, cols], y[:])
+            y_bf16 = sb.tile([P, CHUNK, PACK], BF16, name="y_bf16_%d" % c, align_bytes=64)
+            nc.scalar.copy(
+                y_bf16[:].rearrange("p (a i) t -> p a t i", i=4), y[:].rearrange("p t (a i) -> p a t i", i=4)
+            )
+            return y_bf16
+
+        def planes(c, y_bf16):
+            cols = slice(c * CHUNK, (c + 1) * CHUNK)
+            nc.vector.quantize_mx(
+                y_codes[:, cols].bitcast(FP8X4), y_scales[:, cols], y_bf16[:].rearrange("p j t -> p (j t)")
+            )
+            nc.sync.dma_start(out_words[:, cols], y_codes[:, cols].bitcast(I32))
+
+        hiddens = [hidden(0), hidden(1)]
+        w3_q = quantize_weight("w3", w3_raw, P)
+        hiddens = hiddens + [hidden(2), hidden(3)]
+        diffs = [difference(c, hiddens[c][0]) for c in range(CHUNKS)]
+        gates = [gate(c, hiddens[c][1], hiddens[c][2]) for c in range(CHUNKS)]
+        steps = [update(0, gates[0], diffs[0])]
+        rounded = []
+        for c in range(CHUNKS):
+            if c + 1 < CHUNKS:
+                steps.append(update(c + 1, gates[c + 1], diffs[c + 1]))
+            rounded.append(finish(c, steps[c]))
+            if c > 0:
+                planes(c - 1, rounded[c - 1])
+        planes(CHUNKS - 1, rounded[CHUNKS - 1])
+        for q in range(4):
+            queue = nc.sync if q % 2 == 0 else nc.scalar
+            queue.dma_start(
+                out_2[0, 4 * q : 4 * q + 4, :].bitcast(I32), y_scales[32 * q : 32 * q + 4, :].bitcast(I32)
+            )

@@ -54,7 +54,7 @@ def tile_picked_zhwy_relu_po_kernel(
             return table
 
         def load_weight(name, w, o):
-            raw = sb.tile([P, PACK, H], F32, name=name, align_bytes=64)
+            raw = sb.tile([P, PACK, H], F32, name=name, tag=name, align_bytes=64)
             nc.sync.dma_start(raw[:], w[o * K_PASS : (o + 1) * K_PASS, :].rearrange("(p j) c -> p j c", j=PACK))
             return raw
 
@@ -77,15 +77,18 @@ def tile_picked_zhwy_relu_po_kernel(
                 )
             return picked
 
-        def quantize_weight(name, raw, scalar_share):
+        def round_weight(name, raw, scalar_share):
             grouped = sb.tile([P, PACK, P, PACK], BF16, name=name + "_bf16", align_bytes=64)
-            codes = sb.tile([P, H], U32, name=name + "_codes", align_bytes=64)
-            scales = sb.tile([P, H], U8, name=name + "_scales", align_bytes=64)
             src = raw[:].rearrange("p j (m t) -> p m j t", t=PACK)
             dst = grouped[:].rearrange("p t m j -> p m j t")
             nc.scalar.copy(dst[:, :scalar_share], src[:, :scalar_share])
             if scalar_share < P:
                 nc.vector.tensor_copy(dst[:, scalar_share:], src[:, scalar_share:])
+            return grouped
+
+        def quantize_weight(name, grouped):
+            codes = sb.tile([P, H], U32, name=name + "_codes", align_bytes=64)
+            scales = sb.tile([P, H], U8, name=name + "_scales", align_bytes=64)
             nc.vector.quantize_mx(codes[:].bitcast(FP8X4), scales[:], grouped[:].rearrange("p t m j -> p (t m j)"))
             return codes, scales
 
@@ -111,18 +114,18 @@ def tile_picked_zhwy_relu_po_kernel(
         x_codes0 = gather("x_codes0", x_table0, offs_list, U32, 1)
         x_picked_scales = gather("x_picked_scales", x_scale_table, offs_list, U8, 1)
         x_codes1 = gather("x_codes1", x_table1, offs_list, U32, 1)
-        w1_q0 = quantize_weight("w1_0", w1_raw0, P)
+        w1_q0 = quantize_weight("w1_0", round_weight("w1_0", w1_raw0, P))
         e_picked_scales = gather("e_picked_scales", e_scale_table, tok_list, U8, 1)
         e_codes0 = gather("e_codes0", e_table0, tok_list, U32, 1)
-        w1_q1 = quantize_weight("w1_1", w1_raw1, P)
-        w2_q0 = quantize_weight("w2_0", w2_raw0, SCALAR_SHARE)
-        w2_q1 = quantize_weight("w2_1", w2_raw1, SCALAR_SHARE)
+        w1_q1 = quantize_weight("w1_1", round_weight("w1_1", w1_raw1, P))
+        w2_q0 = quantize_weight("w2_0", round_weight("w2_0", w2_raw0, SCALAR_SHARE))
+        w2_q1 = quantize_weight("w2_1", round_weight("w2_1", w2_raw1, SCALAR_SHARE))
         e_codes1 = gather("e_codes1", e_table1, tok_list, U32, CHUNKS)
 
         passes = [
+            (w2_q0, e_codes0, e_picked_scales, 0),
             (w1_q0, x_codes0, x_picked_scales, 0),
             (w1_q1, x_codes1, x_picked_scales, 1),
-            (w2_q0, e_codes0, e_picked_scales, 0),
             (w2_q1, e_codes1, e_picked_scales, 1),
         ]
 
@@ -150,7 +153,8 @@ def tile_picked_zhwy_relu_po_kernel(
                         start=(i == 0),
                         stop=(i == len(passes) - 1),
                     )
-            h_bf16 = sb.tile([P, CHUNK, PACK], BF16, name="h_bf16_%d" % c, align_bytes=64)
+            name = "h_bf16_%d" % c
+            h_bf16 = sb.tile([P, CHUNK, PACK], BF16, name=name, tag="w3_raw" if c == 1 else name, align_bytes=64)
             nc.scalar.activation(h_bf16[:], acc[:].rearrange("p t j -> p j t"), ACT.Relu)
             h_codes = sb.tile([P, CHUNK], U32, name="h_codes%d" % c, align_bytes=64)
             h_scales = sb.tile([P, CHUNK], U8, name="h_scales%d" % c, align_bytes=64)
@@ -180,45 +184,55 @@ def tile_picked_zhwy_relu_po_kernel(
             nc.scalar.activation(g[:], logits[:], ACT.Sigmoid)
             return g
 
-        def update(c, g, diff):
-            step = sb.tile([P, PACK, CHUNK], F32, name="step%d" % c, align_bytes=64)
-            nc.vector.tensor_tensor(step[:], g[:], diff[:], ALU.mult)
+        def update(c, part, g, diff):
+            step = sb.tile([P, PACK, part.stop - part.start], F32, name="step%d_%d" % (c, part.start), align_bytes=64)
+            nc.vector.tensor_tensor(step[:], g[:, :, part], diff[:, :, part], ALU.mult)
             return step
 
-        def finish(c, step):
-            cols = slice(c * CHUNK, (c + 1) * CHUNK)
-            y = sb.tile([P, PACK, CHUNK], F32, name="y%d" % c, align_bytes=64)
-            nc.vector.tensor_tensor(y[:], step[:], carried_chunk(c), ALU.add)
-            nc.sync.dma_start(out_rows[:, :, cols], y[:])
-            y_bf16 = sb.tile([P, CHUNK, PACK], BF16, name="y_bf16_%d" % c, align_bytes=64)
+        def finish(c, part, step, y):
+            width = part.stop - part.start
+            nc.vector.tensor_tensor(y[:, :, part], step[:], carried_chunk(c)[:, :, part], ALU.add)
+            if part.stop == CHUNK:
+                nc.sync.dma_start(out_rows[:, :, c * CHUNK : (c + 1) * CHUNK], y[:])
+            y_bf16 = sb.tile([P, width, PACK], BF16, name="y_bf16_%d_%d" % (c, part.start), align_bytes=64)
             nc.scalar.copy(
-                y_bf16[:].rearrange("p (a i) t -> p a t i", i=4), y[:].rearrange("p t (a i) -> p a t i", i=4)
+                y_bf16[:].rearrange("p (a i) t -> p a t i", i=4), y[:, :, part].rearrange("p t (a i) -> p a t i", i=4)
             )
             return y_bf16
 
-        def planes(c, y_bf16):
-            cols = slice(c * CHUNK, (c + 1) * CHUNK)
+        def planes(c, part, y_bf16):
+            cols = slice(c * CHUNK + part.start, c * CHUNK + part.stop)
             nc.vector.quantize_mx(
                 y_codes[:, cols].bitcast(FP8X4), y_scales[:, cols], y_bf16[:].rearrange("p j t -> p (j t)")
             )
-            nc.sync.dma_start(out_words[:, cols], y_codes[:, cols].bitcast(I32))
+            if cols.stop == S - CHUNK:
+                nc.sync.dma_start(out_words[:, : cols.stop], y_codes[:, : cols.stop].bitcast(I32))
 
-        hiddens = [hidden(0), hidden(1)]
-        w3_q = quantize_weight("w3", w3_raw, P)
-        hiddens = hiddens + [hidden(2), hidden(3)]
-        diffs = [difference(c, hiddens[c][0]) for c in range(CHUNKS)]
-        gates = [gate(c, hiddens[c][1], hiddens[c][2]) for c in range(CHUNKS)]
-        steps = [update(0, gates[0], diffs[0])]
-        rounded = []
+        hiddens = [hidden(0)]
+        w3_q = quantize_weight("w3", round_weight("w3", w3_raw, SCALAR_SHARE))
+        gates, diffs = [], []
         for c in range(CHUNKS):
+            gates.append(gate(c, hiddens[c][1], hiddens[c][2]))
             if c + 1 < CHUNKS:
-                steps.append(update(c + 1, gates[c + 1], diffs[c + 1]))
-            rounded.append(finish(c, steps[c]))
-            if c > 0:
-                planes(c - 1, rounded[c - 1])
-        planes(CHUNKS - 1, rounded[CHUNKS - 1])
+                hiddens.append(hidden(c + 1))
+            diffs.append(difference(c, hiddens[c][0]))
+        ys = [sb.tile([P, PACK, CHUNK], F32, name="y%d" % c, align_bytes=64) for c in range(CHUNKS)]
+        pieces = [(c, slice(0, CHUNK)) for c in range(CHUNKS - 1)]
+        pieces = pieces + [(CHUNKS - 1, slice(0, CHUNK // 2)), (CHUNKS - 1, slice(CHUNK // 2, CHUNK))]
+        steps, rounded = [], []
+        for i in range(len(pieces) + 2):
+            if i < len(pieces):
+                c, part = pieces[i]
+                steps.append(update(c, part, gates[c], diffs[c]))
+            if 0 <= i - 1 < len(pieces):
+                c, part = pieces[i - 1]
+                rounded.append(finish(c, part, steps[i - 1], ys[c]))
+            if 0 <= i - 2:
+                c, part = pieces[i - 2]
+                planes(c, part, rounded[i - 2])
+        nc.sync.dma_start(out_words[:, S - CHUNK :], y_codes[:, S - CHUNK :].bitcast(I32))
         for q in range(4):
-            queue = nc.sync if q % 2 == 0 else nc.scalar
+            queue = nc.scalar if q % 2 == 0 else nc.sync
             queue.dma_start(
                 out_2[0, 4 * q : 4 * q + 4, :].bitcast(I32), y_scales[32 * q : 32 * q + 4, :].bitcast(I32)
             )

@@ -43,11 +43,11 @@ def tile_picked_zhwy_relu_po_kernel(
             nc.sync.dma_start(table[:], words[o].rearrange("p n t -> p (n t)").bitcast(I32))
             return table
 
-        def load_scales(name, scales):
+        def load_scales(name, scales, clear):
             table = sb.tile([P, T], U8, name=name, align_bytes=64)
-            nc.gpsimd.memset(table[:].bitcast(I32), 0)
+            clear(table[:].bitcast(I32), 0)
             for q in range(4):
-                nc.sync.dma_start(
+                nc.gpsimd.dma_start(
                     table[32 * q : 32 * q + 4 * PASSES, :].bitcast(I32),
                     scales.bitcast(I32)[:, 4 * q : 4 * q + 4, :],
                 )
@@ -81,7 +81,7 @@ def tile_picked_zhwy_relu_po_kernel(
             grouped = sb.tile([P, PACK, P, PACK], BF16, name=name + "_bf16", align_bytes=64)
             src = raw[:].rearrange("p j (m t) -> p m j t", t=PACK)
             dst = grouped[:].rearrange("p t m j -> p m j t")
-            nc.scalar.copy(dst[:, :scalar_share], src[:, :scalar_share])
+            nc.scalar.activation(dst[:, :scalar_share], src[:, :scalar_share], ACT.Copy)
             if scalar_share < P:
                 nc.vector.tensor_copy(dst[:, scalar_share:], src[:, scalar_share:])
             return grouped
@@ -92,16 +92,12 @@ def tile_picked_zhwy_relu_po_kernel(
             nc.vector.quantize_mx(codes[:].bitcast(FP8X4), scales[:], grouped[:].rearrange("p t m j -> p (t m j)"))
             return codes, scales
 
-        warm = sb.tile([P, 8], F32, name="warm")
-        nc.vector.memset(warm[:, 0:1], 0.0)
-        nc.scalar.activation(warm[:, 4:5], warm[:, 0:1], ACT.Sigmoid)
-
         x_table0 = load_words("x_table0", x_words, 0)
         offs_list = load_list("offs_list", offs)
-        x_scale_table = load_scales("x_scale_table", x_scales)
+        x_scale_table = load_scales("x_scale_table", x_scales, nc.gpsimd.memset)
         w1_raw0 = load_weight("w1_raw0", w1, 0)
         tok_list = load_list("tok_list", tok)
-        e_scale_table = load_scales("e_scale_table", e_scales)
+        e_scale_table = load_scales("e_scale_table", e_scales, nc.vector.memset)
         x_table1 = load_words("x_table1", x_words, 1)
         w1_raw1 = load_weight("w1_raw1", w1, 1)
         e_table0 = load_words("e_table0", e_words, 0)
@@ -181,17 +177,17 @@ def tile_picked_zhwy_relu_po_kernel(
                     stop=True,
                 )
             g = sb.tile([P, PACK, CHUNK], F32, name="gate%d" % c, align_bytes=64)
-            nc.scalar.activation(g[:], logits[:], ACT.Sigmoid)
+            nc.scalar.activation(g[:], logits[:], ACT.Tanh, scale=0.5)
             return g
 
         def update(c, part, g, diff):
             step = sb.tile([P, PACK, part.stop - part.start], F32, name="step%d_%d" % (c, part.start), align_bytes=64)
-            nc.vector.tensor_tensor(step[:], g[:, :, part], diff[:, :, part], ALU.mult)
+            nc.vector.scalar_tensor_tensor(step[:], g[:, :, part], 1.0, diff[:, :, part], ALU.add, ALU.mult)
             return step
 
         def finish(c, part, step, y):
             width = part.stop - part.start
-            nc.vector.tensor_tensor(y[:, :, part], step[:], carried_chunk(c)[:, :, part], ALU.add)
+            nc.vector.scalar_tensor_tensor(y[:, :, part], step[:], 0.5, carried_chunk(c)[:, :, part], ALU.mult, ALU.add)
             if part.stop == CHUNK:
                 nc.sync.dma_start(out_rows[:, :, c * CHUNK : (c + 1) * CHUNK], y[:])
             y_bf16 = sb.tile([P, width, PACK], BF16, name="y_bf16_%d_%d" % (c, part.start), align_bytes=64)

@@ -23,6 +23,7 @@ CHUNK = 128
 CHUNKS = S // CHUNK
 LIST_ROWS = 16
 SCALAR_SHARE = 48
+EARLY_SHARE = 96
 
 
 def tile_picked_zhwy_relu_po_kernel(
@@ -47,7 +48,7 @@ def tile_picked_zhwy_relu_po_kernel(
             table = sb.tile([P, T], U8, name=name, align_bytes=64)
             clear(table[:].bitcast(I32), 0)
             for q in range(4):
-                nc.gpsimd.dma_start(
+                nc.sync.dma_start(
                     table[32 * q : 32 * q + 4 * PASSES, :].bitcast(I32),
                     scales.bitcast(I32)[:, 4 * q : 4 * q + 4, :],
                 )
@@ -82,8 +83,7 @@ def tile_picked_zhwy_relu_po_kernel(
             src = raw[:].rearrange("p j (m t) -> p m j t", t=PACK)
             dst = grouped[:].rearrange("p t m j -> p m j t")
             nc.scalar.activation(dst[:, :scalar_share], src[:, :scalar_share], ACT.Copy)
-            if scalar_share < P:
-                nc.vector.tensor_copy(dst[:, scalar_share:], src[:, scalar_share:])
+            nc.vector.tensor_copy(dst[:, scalar_share:], src[:, scalar_share:])
             return grouped
 
         def quantize_weight(name, grouped):
@@ -110,10 +110,10 @@ def tile_picked_zhwy_relu_po_kernel(
         x_codes0 = gather("x_codes0", x_table0, offs_list, U32, 1)
         x_picked_scales = gather("x_picked_scales", x_scale_table, offs_list, U8, 1)
         x_codes1 = gather("x_codes1", x_table1, offs_list, U32, 1)
-        w1_q0 = quantize_weight("w1_0", round_weight("w1_0", w1_raw0, P))
+        w1_q0 = quantize_weight("w1_0", round_weight("w1_0", w1_raw0, EARLY_SHARE))
         e_picked_scales = gather("e_picked_scales", e_scale_table, tok_list, U8, 1)
         e_codes0 = gather("e_codes0", e_table0, tok_list, U32, 1)
-        w1_q1 = quantize_weight("w1_1", round_weight("w1_1", w1_raw1, P))
+        w1_q1 = quantize_weight("w1_1", round_weight("w1_1", w1_raw1, EARLY_SHARE))
         w2_q0 = quantize_weight("w2_0", round_weight("w2_0", w2_raw0, SCALAR_SHARE))
         w2_q1 = quantize_weight("w2_1", round_weight("w2_1", w2_raw1, SCALAR_SHARE))
         e_codes1 = gather("e_codes1", e_table1, tok_list, U32, CHUNKS)
@@ -134,27 +134,36 @@ def tile_picked_zhwy_relu_po_kernel(
             per_half = CHUNKS // 2
             return carried[c // per_half][:, :, (c % per_half) * CHUNK : (c % per_half + 1) * CHUNK]
 
-        def hidden(c):
+        accs = [psum.tile([P, PACK, CHUNK], F32, name="acc%d" % c) for c in range(CHUNKS)]
+
+        def joint_pass(c, t, i):
+            (w_codes, w_scales), codes, scales, o = passes[i]
             cols = slice(c * CHUNK, (c + 1) * CHUNK)
-            acc = psum.tile([P, PACK, CHUNK], F32, name="acc%d" % c)
-            for t in range(PACK):
-                rows = slice(t * P, (t + 1) * P)
-                for i, ((w_codes, w_scales), codes, scales, o) in enumerate(passes):
-                    nc.tensor.matmul_mx(
-                        acc[:, t, :],
-                        lhsT=w_codes[:, rows].bitcast(FP8X4),
-                        lhsT_scale=w_scales[:, rows],
-                        rhs=codes[:, cols].bitcast(FP8X4),
-                        rhs_scale=scales[4 * o :, cols],
-                        start=(i == 0),
-                        stop=(i == len(passes) - 1),
-                    )
-            name = "h_bf16_%d" % c
-            h_bf16 = sb.tile([P, CHUNK, PACK], BF16, name=name, tag="w3_raw" if c == 1 else name, align_bytes=64)
-            nc.scalar.activation(h_bf16[:], acc[:].rearrange("p t j -> p j t"), ACT.Relu)
+            rows = slice(t * P, (t + 1) * P)
+            nc.tensor.matmul_mx(
+                accs[c][:, t, :],
+                lhsT=w_codes[:, rows].bitcast(FP8X4),
+                lhsT_scale=w_scales[:, rows],
+                rhs=codes[:, cols].bitcast(FP8X4),
+                rhs_scale=scales[4 * o :, cols],
+                start=(i == 0),
+                stop=(i == len(passes) - 1),
+            )
+
+        for c in range(CHUNKS):
+            for i in range(len(passes) - 1):
+                joint_pass(c, 0, i)
+
+        def hidden(c):
+            acc = accs[c]
+            joint_pass(c, 0, len(passes) - 1)
+            for t in range(1, PACK):
+                for i in range(len(passes)):
+                    joint_pass(c, t, i)
+            nc.scalar.activation(h_bf16[:, c], acc[:].rearrange("p t j -> p j t"), ACT.Relu)
             h_codes = sb.tile([P, CHUNK], U32, name="h_codes%d" % c, align_bytes=64)
             h_scales = sb.tile([P, CHUNK], U8, name="h_scales%d" % c, align_bytes=64)
-            nc.vector.quantize_mx(h_codes[:].bitcast(FP8X4), h_scales[:], h_bf16[:].rearrange("p j t -> p (j t)"))
+            nc.vector.quantize_mx(h_codes[:].bitcast(FP8X4), h_scales[:], h_bf16[:, c].rearrange("p j t -> p (j t)"))
             return acc, h_codes, h_scales
 
         def difference(c, acc):
@@ -204,13 +213,15 @@ def tile_picked_zhwy_relu_po_kernel(
             if cols.stop == S - CHUNK:
                 nc.sync.dma_start(out_words[:, : cols.stop], y_codes[:, : cols.stop].bitcast(I32))
 
-        hiddens = [hidden(0)]
         w3_q = quantize_weight("w3", round_weight("w3", w3_raw, SCALAR_SHARE))
+        h_bf16 = sb.tile([P, CHUNKS, CHUNK, PACK], BF16, name="h_bf16", tag="w3_raw", align_bytes=64)
+        hiddens = [hidden(0)]
         gates, diffs = [], []
         for c in range(CHUNKS):
             gates.append(gate(c, hiddens[c][1], hiddens[c][2]))
             if c + 1 < CHUNKS:
                 hiddens.append(hidden(c + 1))
+        for c in range(CHUNKS):
             diffs.append(difference(c, hiddens[c][0]))
         ys = [sb.tile([P, PACK, CHUNK], F32, name="y%d" % c, align_bytes=64) for c in range(CHUNKS)]
         pieces = [(c, slice(0, CHUNK)) for c in range(CHUNKS - 1)]

@@ -44,9 +44,9 @@ def tile_picked_zhwy_relu_po_kernel(
             nc.sync.dma_start(table[:], words[o].rearrange("p n t -> p (n t)").bitcast(I32))
             return table
 
-        def load_scales(name, scales, clear):
+        def load_scales(name, scales):
             table = sb.tile([P, T], U8, name=name, align_bytes=64)
-            clear(table[:].bitcast(I32), 0)
+            nc.vector.memset(table[:].bitcast(I32), 0)
             for q in range(4):
                 nc.sync.dma_start(
                     table[32 * q : 32 * q + 4 * PASSES, :].bitcast(I32),
@@ -94,11 +94,11 @@ def tile_picked_zhwy_relu_po_kernel(
 
         x_table0 = load_words("x_table0", x_words, 0)
         offs_list = load_list("offs_list", offs)
-        x_scale_table = load_scales("x_scale_table", x_scales, nc.gpsimd.memset)
+        x_scale_table = load_scales("x_scale_table", x_scales)
         w1_raw0 = load_weight("w1_raw0", w1, 0)
-        tok_list = load_list("tok_list", tok)
-        e_scale_table = load_scales("e_scale_table", e_scales, nc.vector.memset)
         x_table1 = load_words("x_table1", x_words, 1)
+        tok_list = load_list("tok_list", tok)
+        e_scale_table = load_scales("e_scale_table", e_scales)
         w1_raw1 = load_weight("w1_raw1", w1, 1)
         e_table0 = load_words("e_table0", e_words, 0)
         w2_raw0 = load_weight("w2_raw0", w2, 0)

@@ -24,6 +24,7 @@ CHUNKS = S // CHUNK
 LIST_ROWS = 16
 SCALAR_SHARE = 48
 EARLY_SHARE = 96
+W3_SHARE = 20
 
 
 def tile_picked_zhwy_relu_po_kernel(
@@ -59,6 +60,14 @@ def tile_picked_zhwy_relu_po_kernel(
             nc.sync.dma_start(raw[:], w[o * K_PASS : (o + 1) * K_PASS, :].rearrange("(p j) c -> p j c", j=PACK))
             return raw
 
+        def load_weight_columns(name, w, half):
+            width = H // 2
+            raw = sb.tile([P, PACK, width], F32, name=name, tag=name, align_bytes=64)
+            nc.sync.dma_start(
+                raw[:], w[:, half * width : (half + 1) * width].rearrange("(p j) c -> p j c", j=PACK)
+            )
+            return raw
+
         def load_skip(half):
             width = S // 2
             carried = sb.tile([P, PACK, width], F32, name="skip%d" % half, align_bytes=64)
@@ -86,6 +95,16 @@ def tile_picked_zhwy_relu_po_kernel(
             nc.vector.tensor_copy(dst[:, scalar_share:], src[:, scalar_share:])
             return grouped
 
+        def round_weight_halves(name, front, back, scalar_share):
+            grouped = sb.tile([P, PACK, P, PACK], BF16, name=name + "_bf16", align_bytes=64)
+            dst = grouped[:].rearrange("p t m j -> p m j t")
+            mid = P // 2
+            nc.scalar.activation(dst[:, :mid], front[:].rearrange("p j (m t) -> p m j t", t=PACK), ACT.Copy)
+            src = back[:].rearrange("p j (m t) -> p m j t", t=PACK)
+            nc.scalar.activation(dst[:, mid : mid + scalar_share], src[:, :scalar_share], ACT.Copy)
+            nc.vector.tensor_copy(dst[:, mid + scalar_share :], src[:, scalar_share:])
+            return grouped
+
         def quantize_weight(name, grouped):
             codes = sb.tile([P, H], U32, name=name + "_codes", align_bytes=64)
             scales = sb.tile([P, H], U8, name=name + "_scales", align_bytes=64)
@@ -104,7 +123,8 @@ def tile_picked_zhwy_relu_po_kernel(
         w2_raw0 = load_weight("w2_raw0", w2, 0)
         w2_raw1 = load_weight("w2_raw1", w2, 1)
         e_table1 = load_words("e_table1", e_words, 1)
-        w3_raw = load_weight("w3_raw", w3, 0)
+        w3_front = load_weight_columns("w3_front", w3, 0)
+        w3_back = load_weight_columns("w3_back", w3, 1)
         carried = [load_skip(0), load_skip(1)]
 
         x_codes0 = gather("x_codes0", x_table0, offs_list, U32, 1)
@@ -195,13 +215,30 @@ def tile_picked_zhwy_relu_po_kernel(
             return step
 
         def finish(c, part, step, y):
-            width = part.stop - part.start
             nc.vector.scalar_tensor_tensor(y[:, :, part], step[:], 0.5, carried_chunk(c)[:, :, part], ALU.mult, ALU.add)
             if part.stop == CHUNK:
                 nc.sync.dma_start(out_rows[:, :, c * CHUNK : (c + 1) * CHUNK], y[:])
-            y_bf16 = sb.tile([P, width, PACK], BF16, name="y_bf16_%d_%d" % (c, part.start), align_bytes=64)
+
+        def rounded_tile(c, part):
+            width = part.stop - part.start
+            return sb.tile([P, width, PACK], BF16, name="y_bf16_%d_%d" % (c, part.start), align_bytes=64)
+
+        def round_result(c, part, y):
+            y_bf16 = rounded_tile(c, part)
             nc.scalar.copy(
                 y_bf16[:].rearrange("p (a i) t -> p a t i", i=4), y[:, :, part].rearrange("p t (a i) -> p a t i", i=4)
+            )
+            return y_bf16
+
+        def finish_rounded(c, part, step):
+            y_bf16 = rounded_tile(c, part)
+            nc.vector.scalar_tensor_tensor(
+                y_bf16[:],
+                step[:].rearrange("p t j -> p j t"),
+                0.5,
+                carried_chunk(c)[:, :, part].rearrange("p t j -> p j t"),
+                ALU.mult,
+                ALU.add,
             )
             return y_bf16
 
@@ -210,11 +247,12 @@ def tile_picked_zhwy_relu_po_kernel(
             nc.vector.quantize_mx(
                 y_codes[:, cols].bitcast(FP8X4), y_scales[:, cols], y_bf16[:].rearrange("p j t -> p (j t)")
             )
-            if cols.stop == S - CHUNK:
-                nc.sync.dma_start(out_words[:, : cols.stop], y_codes[:, : cols.stop].bitcast(I32))
 
-        w3_q = quantize_weight("w3", round_weight("w3", w3_raw, SCALAR_SHARE))
-        h_bf16 = sb.tile([P, CHUNKS, CHUNK, PACK], BF16, name="h_bf16", tag="w3_raw", align_bytes=64)
+        def store_words(start, stop):
+            nc.sync.dma_start(out_words[:, start:stop], y_codes[:, start:stop].bitcast(I32))
+
+        w3_q = quantize_weight("w3", round_weight_halves("w3", w3_front, w3_back, W3_SHARE))
+        h_bf16 = sb.tile([P, CHUNKS, CHUNK, PACK], BF16, name="h_bf16", tag="w3_back", align_bytes=64)
         hiddens = [hidden(0)]
         gates, diffs = [], []
         for c in range(CHUNKS):
@@ -224,20 +262,27 @@ def tile_picked_zhwy_relu_po_kernel(
         for c in range(CHUNKS):
             diffs.append(difference(c, hiddens[c][0]))
         ys = [sb.tile([P, PACK, CHUNK], F32, name="y%d" % c, align_bytes=64) for c in range(CHUNKS)]
-        pieces = [(c, slice(0, CHUNK)) for c in range(CHUNKS - 1)]
-        pieces = pieces + [(CHUNKS - 1, slice(0, CHUNK // 2)), (CHUNKS - 1, slice(CHUNK // 2, CHUNK))]
+        whole, front, back = slice(0, CHUNK), slice(0, CHUNK // 2), slice(CHUNK // 2, CHUNK)
+        last = CHUNKS - 1
+        pieces = [(c, whole) for c in range(last)] + [(last, front), (last, back)]
         steps, rounded = [], []
-        for i in range(len(pieces) + 2):
-            if i < len(pieces):
-                c, part = pieces[i]
-                steps.append(update(c, part, gates[c], diffs[c]))
-            if 0 <= i - 1 < len(pieces):
+        for i in range(len(pieces)):
+            c, part = pieces[i]
+            steps.append(update(c, part, gates[c], diffs[c]))
+            if 0 <= i - 1:
                 c, part = pieces[i - 1]
-                rounded.append(finish(c, part, steps[i - 1], ys[c]))
-            if 0 <= i - 2:
+                finish(c, part, steps[i - 1], ys[c])
+                rounded.append(round_result(c, part, ys[c]))
+            if 0 <= i - 2 < 2:
                 c, part = pieces[i - 2]
                 planes(c, part, rounded[i - 2])
-        nc.sync.dma_start(out_words[:, S - CHUNK :], y_codes[:, S - CHUNK :].bitcast(I32))
+        store_words(0, S // 2)
+        finish(last, back, steps[-1], ys[last])
+        rounded.append(finish_rounded(last, back, steps[-1]))
+        for i in range(2, len(pieces)):
+            c, part = pieces[i]
+            planes(c, part, rounded[i])
+        store_words(S // 2, S)
         for q in range(4):
             queue = nc.scalar if q % 2 == 0 else nc.sync
             queue.dma_start(

@@ -76,15 +76,15 @@ def tile_picked_zhwy_relu_po_kernel(
             )
             return carried
 
+        def gather_columns(picked, table, lst, dtype, start, stop):
+            nc.vector.tensor_copy(
+                picked[:, start:stop],
+                table[:].bitcast(dtype).indirect(lst[:, start // LIST_ROWS : stop // LIST_ROWS]),
+            )
+
         def gather(name, table, lst, dtype, pieces):
             picked = sb.tile([P, S], dtype, name=name, align_bytes=64)
-            width = S // pieces
-            cols = width // LIST_ROWS
-            for c in range(pieces):
-                nc.vector.tensor_copy(
-                    picked[:, c * width : (c + 1) * width],
-                    table[:].bitcast(dtype).indirect(lst[:, c * cols : (c + 1) * cols]),
-                )
+            gather_columns(picked, table, lst, dtype, 0, S)
             return picked
 
         def round_weight(name, raw, scalar_share):
@@ -135,8 +135,21 @@ def tile_picked_zhwy_relu_po_kernel(
         e_codes0 = gather("e_codes0", e_table0, tok_list, U32, 1)
         w1_q1 = quantize_weight("w1_1", round_weight("w1_1", w1_raw1, EARLY_SHARE))
         w2_q0 = quantize_weight("w2_0", round_weight("w2_0", w2_raw0, SCALAR_SHARE))
-        w2_q1 = quantize_weight("w2_1", round_weight("w2_1", w2_raw1, SCALAR_SHARE))
-        e_codes1 = gather("e_codes1", e_table1, tok_list, U32, CHUNKS)
+        w2_bf16 = round_weight("w2_1", w2_raw1, SCALAR_SHARE)
+        e_codes1 = sb.tile([P, S], U32, name="e_codes1", align_bytes=64)
+        gather_columns(e_codes1, e_table1, tok_list, U32, 0, CHUNK)
+        w2_codes = sb.tile([P, H], U32, name="w2_1_codes", align_bytes=64)
+        w2_scales = sb.tile([P, H], U8, name="w2_1_scales", align_bytes=64)
+        for u in range(2):
+            rows = slice(u * H // 2, (u + 1) * H // 2)
+            nc.vector.quantize_mx(
+                w2_codes[:, rows].bitcast(FP8X4),
+                w2_scales[:, rows],
+                w2_bf16[:, 2 * u : 2 * u + 2].rearrange("p t m j -> p (t m j)"),
+            )
+        w2_q1 = (w2_codes, w2_scales)
+        for c in range(1, CHUNKS):
+            gather_columns(e_codes1, e_table1, tok_list, U32, c * CHUNK, (c + 1) * CHUNK)
 
         passes = [
             (w2_q0, e_codes0, e_picked_scales, 0),
@@ -264,24 +277,24 @@ def tile_picked_zhwy_relu_po_kernel(
         ys = [sb.tile([P, PACK, CHUNK], F32, name="y%d" % c, align_bytes=64) for c in range(CHUNKS)]
         whole, front, back = slice(0, CHUNK), slice(0, CHUNK // 2), slice(CHUNK // 2, CHUNK)
         last = CHUNKS - 1
-        pieces = [(c, whole) for c in range(last)] + [(last, front), (last, back)]
-        steps, rounded = [], []
-        for i in range(len(pieces)):
-            c, part = pieces[i]
-            steps.append(update(c, part, gates[c], diffs[c]))
-            if 0 <= i - 1:
-                c, part = pieces[i - 1]
-                finish(c, part, steps[i - 1], ys[c])
-                rounded.append(round_result(c, part, ys[c]))
-            if 0 <= i - 2 < 2:
-                c, part = pieces[i - 2]
-                planes(c, part, rounded[i - 2])
+        steps, rounded = [update(0, whole, gates[0], diffs[0])], []
+        for c in range(last):
+            if c + 1 < last:
+                steps.append(update(c + 1, whole, gates[c + 1], diffs[c + 1]))
+            finish(c, whole, steps[c], ys[c])
+            rounded.append(round_result(c, whole, ys[c]))
+        planes(0, whole, rounded[0])
+        step_front = update(last, front, gates[last], diffs[last])
+        step_back = update(last, back, gates[last], diffs[last])
+        planes(1, whole, rounded[1])
         store_words(0, S // 2)
-        finish(last, back, steps[-1], ys[last])
-        rounded.append(finish_rounded(last, back, steps[-1]))
-        for i in range(2, len(pieces)):
-            c, part = pieces[i]
-            planes(c, part, rounded[i])
+        finish(last, front, step_front, ys[last])
+        rounded_front = round_result(last, front, ys[last])
+        finish(last, back, step_back, ys[last])
+        rounded_back = finish_rounded(last, back, step_back)
+        planes(last - 1, whole, rounded[last - 1])
+        planes(last, front, rounded_front)
+        planes(last, back, rounded_back)
         store_words(S // 2, S)
         for q in range(4):
             queue = nc.scalar if q % 2 == 0 else nc.sync

@@ -23,8 +23,9 @@ CHUNK = 128
 CHUNKS = S // CHUNK
 LIST_ROWS = 16
 SCALAR_SHARE = 48
-EARLY_SHARE = 96
+EARLY_SHARE = 128
 W3_SHARE = 20
+E_ROW = 8
 
 
 def tile_picked_zhwy_relu_po_kernel(
@@ -45,12 +46,12 @@ def tile_picked_zhwy_relu_po_kernel(
             nc.sync.dma_start(table[:], words[o].rearrange("p n t -> p (n t)").bitcast(I32))
             return table
 
-        def load_scales(name, scales):
+        def load_scales(name, scales, first_row, clearing_engine, queue):
             table = sb.tile([P, T], U8, name=name, align_bytes=64)
-            nc.vector.memset(table[:].bitcast(I32), 0)
+            clearing_engine.memset(table[:].bitcast(I32), 0)
             for q in range(4):
-                nc.sync.dma_start(
-                    table[32 * q : 32 * q + 4 * PASSES, :].bitcast(I32),
+                queue.dma_start(
+                    table[32 * q + first_row : 32 * q + first_row + 4 * PASSES, :].bitcast(I32),
                     scales.bitcast(I32)[:, 4 * q : 4 * q + 4, :],
                 )
             return table
@@ -92,7 +93,8 @@ def tile_picked_zhwy_relu_po_kernel(
             src = raw[:].rearrange("p j (m t) -> p m j t", t=PACK)
             dst = grouped[:].rearrange("p t m j -> p m j t")
             nc.scalar.activation(dst[:, :scalar_share], src[:, :scalar_share], ACT.Copy)
-            nc.vector.tensor_copy(dst[:, scalar_share:], src[:, scalar_share:])
+            if scalar_share < P:
+                nc.vector.tensor_copy(dst[:, scalar_share:], src[:, scalar_share:])
             return grouped
 
         def round_weight_halves(name, front, back, scalar_share):
@@ -111,13 +113,13 @@ def tile_picked_zhwy_relu_po_kernel(
             nc.vector.quantize_mx(codes[:].bitcast(FP8X4), scales[:], grouped[:].rearrange("p t m j -> p (t m j)"))
             return codes, scales
 
+        e_scale_table = load_scales("e_scale_table", e_scales, E_ROW, nc.gpsimd, nc.gpsimd)
         x_table0 = load_words("x_table0", x_words, 0)
         offs_list = load_list("offs_list", offs)
-        x_scale_table = load_scales("x_scale_table", x_scales)
+        x_scale_table = load_scales("x_scale_table", x_scales, 0, nc.vector, nc.sync)
         w1_raw0 = load_weight("w1_raw0", w1, 0)
         x_table1 = load_words("x_table1", x_words, 1)
         tok_list = load_list("tok_list", tok)
-        e_scale_table = load_scales("e_scale_table", e_scales)
         w1_raw1 = load_weight("w1_raw1", w1, 1)
         e_table0 = load_words("e_table0", e_words, 0)
         w2_raw0 = load_weight("w2_raw0", w2, 0)
@@ -152,10 +154,10 @@ def tile_picked_zhwy_relu_po_kernel(
             gather_columns(e_codes1, e_table1, tok_list, U32, c * CHUNK, (c + 1) * CHUNK)
 
         passes = [
-            (w2_q0, e_codes0, e_picked_scales, 0),
+            (w2_q0, e_codes0, e_picked_scales, E_ROW),
             (w1_q0, x_codes0, x_picked_scales, 0),
-            (w1_q1, x_codes1, x_picked_scales, 1),
-            (w2_q1, e_codes1, e_picked_scales, 1),
+            (w1_q1, x_codes1, x_picked_scales, 4),
+            (w2_q1, e_codes1, e_picked_scales, E_ROW + 4),
         ]
 
         y_codes = sb.tile([P, S], U32, name="y_codes", align_bytes=64)
@@ -170,7 +172,7 @@ def tile_picked_zhwy_relu_po_kernel(
         accs = [psum.tile([P, PACK, CHUNK], F32, name="acc%d" % c) for c in range(CHUNKS)]
 
         def joint_pass(c, t, i):
-            (w_codes, w_scales), codes, scales, o = passes[i]
+            (w_codes, w_scales), codes, scales, scale_row = passes[i]
             cols = slice(c * CHUNK, (c + 1) * CHUNK)
             rows = slice(t * P, (t + 1) * P)
             nc.tensor.matmul_mx(
@@ -178,7 +180,7 @@ def tile_picked_zhwy_relu_po_kernel(
                 lhsT=w_codes[:, rows].bitcast(FP8X4),
                 lhsT_scale=w_scales[:, rows],
                 rhs=codes[:, cols].bitcast(FP8X4),
-                rhs_scale=scales[4 * o :, cols],
+                rhs_scale=scales[scale_row:, cols],
                 start=(i == 0),
                 stop=(i == len(passes) - 1),
             )

@@ -46,6 +46,11 @@ def tile_picked_zhwy_relu_po_kernel(
             nc.sync.dma_start(table[:], words[o].rearrange("p n t -> p (n t)").bitcast(I32))
             return table
 
+        def load_both_passes(name, words):
+            table = sb.tile([P, PASSES, T], I32, name=name, align_bytes=64)
+            nc.sync.dma_start(table[:], words.rearrange("o p n t -> p o (n t)").bitcast(I32))
+            return table
+
         def load_scales(name, scales, first_row, clearing_engine, queue):
             table = sb.tile([P, T], U8, name=name, align_bytes=64)
             clearing_engine.memset(table[:].bitcast(I32), 0)
@@ -80,7 +85,7 @@ def tile_picked_zhwy_relu_po_kernel(
         def gather_columns(picked, table, lst, dtype, start, stop):
             nc.vector.tensor_copy(
                 picked[:, start:stop],
-                table[:].bitcast(dtype).indirect(lst[:, start // LIST_ROWS : stop // LIST_ROWS]),
+                table.bitcast(dtype).indirect(lst[:, start // LIST_ROWS : stop // LIST_ROWS]),
             )
 
         def gather(name, table, lst, dtype, pieces):
@@ -97,15 +102,23 @@ def tile_picked_zhwy_relu_po_kernel(
                 nc.vector.tensor_copy(dst[:, scalar_share:], src[:, scalar_share:])
             return grouped
 
-        def round_weight_halves(name, front, back, scalar_share):
-            grouped = sb.tile([P, PACK, P, PACK], BF16, name=name + "_bf16", align_bytes=64)
-            dst = grouped[:].rearrange("p t m j -> p m j t")
+        def round_half(name, raw, scalar_share):
             mid = P // 2
-            nc.scalar.activation(dst[:, :mid], front[:].rearrange("p j (m t) -> p m j t", t=PACK), ACT.Copy)
-            src = back[:].rearrange("p j (m t) -> p m j t", t=PACK)
-            nc.scalar.activation(dst[:, mid : mid + scalar_share], src[:, :scalar_share], ACT.Copy)
-            nc.vector.tensor_copy(dst[:, mid + scalar_share :], src[:, scalar_share:])
+            grouped = sb.tile([P, PACK, mid, PACK], BF16, name=name + "_bf16", align_bytes=64)
+            dst = grouped[:].rearrange("p t m j -> p m j t")
+            src = raw[:].rearrange("p j (m t) -> p m j t", t=PACK)
+            nc.scalar.activation(dst[:, :scalar_share], src[:, :scalar_share], ACT.Copy)
+            if scalar_share < mid:
+                nc.vector.tensor_copy(dst[:, scalar_share:], src[:, scalar_share:])
             return grouped
+
+        def quantize_half(grouped, half):
+            mid = P // 2
+            for t in range(PACK):
+                cols = slice(t * P + half * mid, t * P + (half + 1) * mid)
+                nc.vector.quantize_mx(
+                    w3_q[0][:, cols].bitcast(FP8X4), w3_q[1][:, cols], grouped[:, t].rearrange("p m j -> p (m j)")
+                )
 
         def quantize_weight(name, grouped):
             codes = sb.tile([P, H], U32, name=name + "_codes", align_bytes=64)
@@ -114,11 +127,10 @@ def tile_picked_zhwy_relu_po_kernel(
             return codes, scales
 
         e_scale_table = load_scales("e_scale_table", e_scales, E_ROW, nc.gpsimd, nc.gpsimd)
-        x_table0 = load_words("x_table0", x_words, 0)
+        x_table = load_both_passes("x_table", x_words)
         offs_list = load_list("offs_list", offs)
         x_scale_table = load_scales("x_scale_table", x_scales, 0, nc.vector, nc.sync)
         w1_raw0 = load_weight("w1_raw0", w1, 0)
-        x_table1 = load_words("x_table1", x_words, 1)
         tok_list = load_list("tok_list", tok)
         w1_raw1 = load_weight("w1_raw1", w1, 1)
         e_table0 = load_words("e_table0", e_words, 0)
@@ -129,17 +141,17 @@ def tile_picked_zhwy_relu_po_kernel(
         w3_back = load_weight_columns("w3_back", w3, 1)
         carried = [load_skip(0), load_skip(1)]
 
-        x_codes0 = gather("x_codes0", x_table0, offs_list, U32, 1)
-        x_picked_scales = gather("x_picked_scales", x_scale_table, offs_list, U8, 1)
-        x_codes1 = gather("x_codes1", x_table1, offs_list, U32, 1)
+        x_codes0 = gather("x_codes0", x_table[:, 0, :], offs_list, U32, 1)
+        x_codes1 = gather("x_codes1", x_table[:, 1, :], offs_list, U32, 1)
+        x_picked_scales = gather("x_picked_scales", x_scale_table[:], offs_list, U8, 1)
         w1_q0 = quantize_weight("w1_0", round_weight("w1_0", w1_raw0, EARLY_SHARE))
-        e_picked_scales = gather("e_picked_scales", e_scale_table, tok_list, U8, 1)
-        e_codes0 = gather("e_codes0", e_table0, tok_list, U32, 1)
+        e_picked_scales = gather("e_picked_scales", e_scale_table[:], tok_list, U8, 1)
+        e_codes0 = gather("e_codes0", e_table0[:], tok_list, U32, 1)
         w1_q1 = quantize_weight("w1_1", round_weight("w1_1", w1_raw1, EARLY_SHARE))
         w2_q0 = quantize_weight("w2_0", round_weight("w2_0", w2_raw0, SCALAR_SHARE))
         w2_bf16 = round_weight("w2_1", w2_raw1, SCALAR_SHARE)
         e_codes1 = sb.tile([P, S], U32, name="e_codes1", align_bytes=64)
-        gather_columns(e_codes1, e_table1, tok_list, U32, 0, CHUNK)
+        gather_columns(e_codes1, e_table1[:], tok_list, U32, 0, CHUNK)
         w2_codes = sb.tile([P, H], U32, name="w2_1_codes", align_bytes=64)
         w2_scales = sb.tile([P, H], U8, name="w2_1_scales", align_bytes=64)
         for u in range(2):
@@ -151,7 +163,7 @@ def tile_picked_zhwy_relu_po_kernel(
             )
         w2_q1 = (w2_codes, w2_scales)
         for c in range(1, CHUNKS):
-            gather_columns(e_codes1, e_table1, tok_list, U32, c * CHUNK, (c + 1) * CHUNK)
+            gather_columns(e_codes1, e_table1[:], tok_list, U32, c * CHUNK, (c + 1) * CHUNK)
 
         passes = [
             (w2_q0, e_codes0, e_picked_scales, E_ROW),
@@ -266,7 +278,13 @@ def tile_picked_zhwy_relu_po_kernel(
         def store_words(start, stop):
             nc.sync.dma_start(out_words[:, start:stop], y_codes[:, start:stop].bitcast(I32))
 
-        w3_q = quantize_weight("w3", round_weight_halves("w3", w3_front, w3_back, W3_SHARE))
+        w3_codes = sb.tile([P, H], U32, name="w3_codes", align_bytes=64)
+        w3_scales = sb.tile([P, H], U8, name="w3_scales", align_bytes=64)
+        w3_q = (w3_codes, w3_scales)
+        front_bf16 = round_half("w3_front", w3_front, P // 2)
+        back_bf16 = round_half("w3_back", w3_back, W3_SHARE)
+        quantize_half(front_bf16, 0)
+        quantize_half(back_bf16, 1)
         h_bf16 = sb.tile([P, CHUNKS, CHUNK, PACK], BF16, name="h_bf16", tag="w3_back", align_bytes=64)
         hiddens = [hidden(0)]
         gates, diffs = [], []
@@ -295,9 +313,10 @@ def tile_picked_zhwy_relu_po_kernel(
         finish(last, back, step_back, ys[last])
         rounded_back = finish_rounded(last, back, step_back)
         planes(last - 1, whole, rounded[last - 1])
+        store_words(S // 2, last * CHUNK)
         planes(last, front, rounded_front)
         planes(last, back, rounded_back)
-        store_words(S // 2, S)
+        store_words(last * CHUNK, S)
         for q in range(4):
             queue = nc.scalar if q % 2 == 0 else nc.sync
             queue.dma_start(

from contextlib import ExitStack

import concourse.mybir as mybir

K, T, S, H = 1024, 1024, 512, 512
FLOPS = 2 * (2 * K * H * S + H * H * S)

F32 = mybir.dt.float32
BF16 = mybir.dt.bfloat16
I32 = mybir.dt.int32
U32 = mybir.dt.uint32
U16 = mybir.dt.uint16
U8 = mybir.dt.uint8
FP8X4 = mybir.dt.float8_e4m3fn_x4
ACT = mybir.ActivationFunctionType
ALU = mybir.AluOpType

P = 128
PACK = 4
K_PASS = P * PACK
PASSES = K // K_PASS
CHUNK = 128
CHUNKS = S // CHUNK
LIST_ROWS = 16
SCALAR_SHARE = 48
EARLY_SHARE = 128
W3_SHARE = 20
E_ROW = 8


def tile_picked_zhwy_relu_po_kernel(
    tc, x_words, x_scales, e_words, e_scales, w1, w2, w3, skip, offs, tok, out_0, out_1, out_2
):
    nc = tc.nc
    with ExitStack() as ctx:
        sb = ctx.enter_context(tc.tile_pool(name="sb", bufs=1))
        psum = ctx.enter_context(tc.psum_pool(name="psum", bufs=1))

        def load_list(name, src):
            lst = sb.tile([P, S // LIST_ROWS], U16, name=name)
            nc.sync.dma_start(lst[:], src)
            return lst

        def load_words(name, words, o):
            table = sb.tile([P, T], I32, name=name, align_bytes=64)
            nc.sync.dma_start(table[:], words[o].rearrange("p n t -> p (n t)").bitcast(I32))
            return table

        def load_both_passes(name, words):
            table = sb.tile([P, PASSES, T], I32, name=name, align_bytes=64)
            nc.sync.dma_start(table[:], words.rearrange("o p n t -> p o (n t)").bitcast(I32))
            return table

        def load_scales(name, scales, first_row, clearing_engine, queue):
            table = sb.tile([P, T], U8, name=name, align_bytes=64)
            clearing_engine.memset(table[:].bitcast(I32), 0)
            for q in range(4):
                queue.dma_start(
                    table[32 * q + first_row : 32 * q + first_row + 4 * PASSES, :].bitcast(I32),
                    scales.bitcast(I32)[:, 4 * q : 4 * q + 4, :],
                )
            return table

        def load_weight(name, w, o):
            raw = sb.tile([P, PACK, H], F32, name=name, tag=name, align_bytes=64)
            nc.sync.dma_start(raw[:], w[o * K_PASS : (o + 1) * K_PASS, :].rearrange("(p j) c -> p j c", j=PACK))
            return raw

        def load_weight_columns(name, w, half):
            width = H // 2
            raw = sb.tile([P, PACK, width], F32, name=name, tag=name, align_bytes=64)
            nc.sync.dma_start(
                raw[:], w[:, half * width : (half + 1) * width].rearrange("(p j) c -> p j c", j=PACK)
            )
            return raw

        def load_skip(half):
            width = S // 2
            carried = sb.tile([P, PACK, width], F32, name="skip%d" % half, align_bytes=64)
            nc.sync.dma_start(
                carried[:], skip[:, half * width : (half + 1) * width].rearrange("(p t) j -> p t j", t=PACK)
            )
            return carried

        def gather_columns(picked, table, lst, dtype, start, stop):
            nc.vector.tensor_copy(
                picked[:, start:stop],
                table.bitcast(dtype).indirect(lst[:, start // LIST_ROWS : stop // LIST_ROWS]),
            )

        def gather(name, table, lst, dtype, pieces):
            picked = sb.tile([P, S], dtype, name=name, align_bytes=64)
            gather_columns(picked, table, lst, dtype, 0, S)
            return picked

        def round_weight(name, raw, scalar_share):
            grouped = sb.tile([P, PACK, P, PACK], BF16, name=name + "_bf16", align_bytes=64)
            src = raw[:].rearrange("p j (m t) -> p m j t", t=PACK)
            dst = grouped[:].rearrange("p t m j -> p m j t")
            nc.scalar.activation(dst[:, :scalar_share], src[:, :scalar_share], ACT.Copy)
            if scalar_share < P:
                nc.vector.tensor_copy(dst[:, scalar_share:], src[:, scalar_share:])
            return grouped

        def round_half(name, raw, scalar_share):
            mid = P // 2
            grouped = sb.tile([P, PACK, mid, PACK], BF16, name=name + "_bf16", align_bytes=64)
            dst = grouped[:].rearrange("p t m j -> p m j t")
            src = raw[:].rearrange("p j (m t) -> p m j t", t=PACK)
            nc.scalar.activation(dst[:, :scalar_share], src[:, :scalar_share], ACT.Copy)
            if scalar_share < mid:
                nc.vector.tensor_copy(dst[:, scalar_share:], src[:, scalar_share:])
            return grouped

        def quantize_half(grouped, half):
            mid = P // 2
            for t in range(PACK):
                cols = slice(t * P + half * mid, t * P + (half + 1) * mid)
                nc.vector.quantize_mx(
                    w3_q[0][:, cols].bitcast(FP8X4), w3_q[1][:, cols], grouped[:, t].rearrange("p m j -> p (m j)")
                )

        def quantize_weight(name, grouped):
            codes = sb.tile([P, H], U32, name=name + "_codes", align_bytes=64)
            scales = sb.tile([P, H], U8, name=name + "_scales", align_bytes=64)
            nc.vector.quantize_mx(codes[:].bitcast(FP8X4), scales[:], grouped[:].rearrange("p t m j -> p (t m j)"))
            return codes, scales

        e_scale_table = load_scales("e_scale_table", e_scales, E_ROW, nc.gpsimd, nc.gpsimd)
        x_table = load_both_passes("x_table", x_words)
        offs_list = load_list("offs_list", offs)
        x_scale_table = load_scales("x_scale_table", x_scales, 0, nc.vector, nc.sync)
        w1_raw0 = load_weight("w1_raw0", w1, 0)
        tok_list = load_list("tok_list", tok)
        w1_raw1 = load_weight("w1_raw1", w1, 1)
        e_table0 = load_words("e_table0", e_words, 0)
        w2_raw0 = load_weight("w2_raw0", w2, 0)
        w2_raw1 = load_weight("w2_raw1", w2, 1)
        e_table1 = load_words("e_table1", e_words, 1)
        w3_front = load_weight_columns("w3_front", w3, 0)
        w3_back = load_weight_columns("w3_back", w3, 1)
        carried = [load_skip(0), load_skip(1)]

        x_codes0 = gather("x_codes0", x_table[:, 0, :], offs_list, U32, 1)
        x_codes1 = gather("x_codes1", x_table[:, 1, :], offs_list, U32, 1)
        x_picked_scales = gather("x_picked_scales", x_scale_table[:], offs_list, U8, 1)
        w1_q0 = quantize_weight("w1_0", round_weight("w1_0", w1_raw0, EARLY_SHARE))
        e_picked_scales = gather("e_picked_scales", e_scale_table[:], tok_list, U8, 1)
        e_codes0 = gather("e_codes0", e_table0[:], tok_list, U32, 1)
        w1_q1 = quantize_weight("w1_1", round_weight("w1_1", w1_raw1, EARLY_SHARE))
        w2_q0 = quantize_weight("w2_0", round_weight("w2_0", w2_raw0, SCALAR_SHARE))
        w2_bf16 = round_weight("w2_1", w2_raw1, SCALAR_SHARE)
        e_codes1 = sb.tile([P, S], U32, name="e_codes1", align_bytes=64)
        gather_columns(e_codes1, e_table1[:], tok_list, U32, 0, CHUNK)
        w2_codes = sb.tile([P, H], U32, name="w2_1_codes", align_bytes=64)
        w2_scales = sb.tile([P, H], U8, name="w2_1_scales", align_bytes=64)
        for u in range(2):
            rows = slice(u * H // 2, (u + 1) * H // 2)
            nc.vector.quantize_mx(
                w2_codes[:, rows].bitcast(FP8X4),
                w2_scales[:, rows],
                w2_bf16[:, 2 * u : 2 * u + 2].rearrange("p t m j -> p (t m j)"),
            )
        w2_q1 = (w2_codes, w2_scales)
        for c in range(1, CHUNKS):
            gather_columns(e_codes1, e_table1[:], tok_list, U32, c * CHUNK, (c + 1) * CHUNK)

        passes = [
            (w2_q0, e_codes0, e_picked_scales, E_ROW),
            (w1_q0, x_codes0, x_picked_scales, 0),
            (w1_q1, x_codes1, x_picked_scales, 4),
            (w2_q1, e_codes1, e_picked_scales, E_ROW + 4),
        ]

        y_codes = sb.tile([P, S], U32, name="y_codes", align_bytes=64)
        y_scales = sb.tile([P, S], U8, name="y_scales", align_bytes=64)
        out_rows = out_0.rearrange("(p t) j -> p t j", t=PACK)
        out_words = out_1[0].rearrange("p n t -> p (n t)").bitcast(I32)

        def carried_chunk(c):
            per_half = CHUNKS // 2
            return carried[c // per_half][:, :, (c % per_half) * CHUNK : (c % per_half + 1) * CHUNK]

        accs = [psum.tile([P, PACK, CHUNK], F32, name="acc%d" % c) for c in range(CHUNKS)]

        def joint_pass(c, t, i):
            (w_codes, w_scales), codes, scales, scale_row = passes[i]
            cols = slice(c * CHUNK, (c + 1) * CHUNK)
            rows = slice(t * P, (t + 1) * P)
            nc.tensor.matmul_mx(
                accs[c][:, t, :],
                lhsT=w_codes[:, rows].bitcast(FP8X4),
                lhsT_scale=w_scales[:, rows],
                rhs=codes[:, cols].bitcast(FP8X4),
                rhs_scale=scales[scale_row:, cols],
                start=(i == 0),
                stop=(i == len(passes) - 1),
            )

        for c in range(CHUNKS):
            for i in range(len(passes) - 1):
                joint_pass(c, 0, i)

        def hidden(c):
            acc = accs[c]
            joint_pass(c, 0, len(passes) - 1)
            for t in range(1, PACK):
                for i in range(len(passes)):
                    joint_pass(c, t, i)
            nc.scalar.activation(h_bf16[:, c], acc[:].rearrange("p t j -> p j t"), ACT.Relu)
            h_codes = sb.tile([P, CHUNK], U32, name="h_codes%d" % c, align_bytes=64)
            h_scales = sb.tile([P, CHUNK], U8, name="h_scales%d" % c, align_bytes=64)
            nc.vector.quantize_mx(h_codes[:].bitcast(FP8X4), h_scales[:], h_bf16[:, c].rearrange("p j t -> p (j t)"))
            return acc, h_codes, h_scales

        def difference(c, acc):
            diff = sb.tile([P, PACK, CHUNK], F32, name="diff%d" % c, align_bytes=64)
            nc.vector.scalar_tensor_tensor(diff[:], acc[:], 0.0, carried_chunk(c), ALU.max, ALU.subtract)
            return diff

        def gate(c, h_codes, h_scales):
            w_codes, w_scales = w3_q
            logits = psum.tile([P, PACK, CHUNK], F32, name="logits%d" % c)
            for t in range(PACK):
                rows = slice(t * P, (t + 1) * P)
                nc.tensor.matmul_mx(
                    logits[:, t, :],
                    lhsT=w_codes[:, rows].bitcast(FP8X4),
                    lhsT_scale=w_scales[:, rows],
                    rhs=h_codes[:].bitcast(FP8X4),
                    rhs_scale=h_scales[:],
                    start=True,
                    stop=True,
                )
            g = sb.tile([P, PACK, CHUNK], F32, name="gate%d" % c, align_bytes=64)
            nc.scalar.activation(g[:], logits[:], ACT.Tanh, scale=0.5)
            return g

        def update(c, part, g, diff):
            step = sb.tile([P, PACK, part.stop - part.start], F32, name="step%d_%d" % (c, part.start), align_bytes=64)
            nc.vector.scalar_tensor_tensor(step[:], g[:, :, part], 1.0, diff[:, :, part], ALU.add, ALU.mult)
            return step

        def finish(c, part, step, y):
            nc.vector.scalar_tensor_tensor(y[:, :, part], step[:], 0.5, carried_chunk(c)[:, :, part], ALU.mult, ALU.add)
            if part.stop == CHUNK:
                nc.sync.dma_start(out_rows[:, :, c * CHUNK : (c + 1) * CHUNK], y[:])

        def rounded_tile(c, part):
            width = part.stop - part.start
            return sb.tile([P, width, PACK], BF16, name="y_bf16_%d_%d" % (c, part.start), align_bytes=64)

        def round_result(c, part, y):
            y_bf16 = rounded_tile(c, part)
            nc.scalar.copy(
                y_bf16[:].rearrange("p (a i) t -> p a t i", i=4), y[:, :, part].rearrange("p t (a i) -> p a t i", i=4)
            )
            return y_bf16

        def finish_rounded(c, part, step):
            y_bf16 = rounded_tile(c, part)
            nc.vector.scalar_tensor_tensor(
                y_bf16[:],
                step[:].rearrange("p t j -> p j t"),
                0.5,
                carried_chunk(c)[:, :, part].rearrange("p t j -> p j t"),
                ALU.mult,
                ALU.add,
            )
            return y_bf16

        def planes(c, part, y_bf16):
            cols = slice(c * CHUNK + part.start, c * CHUNK + part.stop)
            nc.vector.quantize_mx(
                y_codes[:, cols].bitcast(FP8X4), y_scales[:, cols], y_bf16[:].rearrange("p j t -> p (j t)")
            )

        def store_words(start, stop):
            nc.sync.dma_start(out_words[:, start:stop], y_codes[:, start:stop].bitcast(I32))

        w3_codes = sb.tile([P, H], U32, name="w3_codes", align_bytes=64)
        w3_scales = sb.tile([P, H], U8, name="w3_scales", align_bytes=64)
        w3_q = (w3_codes, w3_scales)
        front_bf16 = round_half("w3_front", w3_front, P // 2)
        back_bf16 = round_half("w3_back", w3_back, W3_SHARE)
        quantize_half(front_bf16, 0)
        quantize_half(back_bf16, 1)
        h_bf16 = sb.tile([P, CHUNKS, CHUNK, PACK], BF16, name="h_bf16", tag="w3_back", align_bytes=64)
        hiddens = [hidden(0)]
        gates, diffs = [], []
        for c in range(CHUNKS):
            gates.append(gate(c, hiddens[c][1], hiddens[c][2]))
            if c + 1 < CHUNKS:
                hiddens.append(hidden(c + 1))
        for c in range(CHUNKS):
            diffs.append(difference(c, hiddens[c][0]))
        ys = [sb.tile([P, PACK, CHUNK], F32, name="y%d" % c, align_bytes=64) for c in range(CHUNKS)]
        whole, front, back = slice(0, CHUNK), slice(0, CHUNK // 2), slice(CHUNK // 2, CHUNK)
        last = CHUNKS - 1
        steps, rounded = [update(0, whole, gates[0], diffs[0])], []
        for c in range(last):
            if c + 1 < last:
                steps.append(update(c + 1, whole, gates[c + 1], diffs[c + 1]))
            finish(c, whole, steps[c], ys[c])
            rounded.append(round_result(c, whole, ys[c]))
        planes(0, whole, rounded[0])
        step_front = update(last, front, gates[last], diffs[last])
        step_back = update(last, back, gates[last], diffs[last])
        planes(1, whole, rounded[1])
        store_words(0, S // 2)
        finish(last, front, step_front, ys[last])
        rounded_front = round_result(last, front, ys[last])
        finish(last, back, step_back, ys[last])
        rounded_back = finish_rounded(last, back, step_back)
        planes(last - 1, whole, rounded[last - 1])
        store_words(S // 2, last * CHUNK)
        planes(last, front, rounded_front)
        planes(last, back, rounded_back)
        store_words(last * CHUNK, S)
        for q in range(4):
            queue = nc.scalar if q % 2 == 0 else nc.sync
            queue.dma_start(
                out_2[0, 4 * q : 4 * q + 4, :].bitcast(I32), y_scales[32 * q : 32 * q + 4, :].bitcast(I32)
            )
